import numpy as np
import ml_dtypes


def mxq(x, axis, fmt="e4m3"):
    dtype, down = {"e4m3": (ml_dtypes.float8_e4m3fn, 7), "e5m2": (ml_dtypes.float8_e5m2, 14)}[fmt]
    v = np.moveaxis(np.asarray(x, np.float32).astype(ml_dtypes.bfloat16).astype(np.float64), axis, -1)
    blocks = v.reshape(v.shape[:-1] + (-1, 32))
    amax = np.abs(blocks).max(-1, keepdims=True)
    byte = np.maximum(np.where(amax > 0, np.frexp(amax)[1] - 1 + 127, 0) - down, 1)
    scale = np.exp2(byte - 127.0)
    codes = (blocks / scale).astype(np.float32).astype(dtype).astype(np.float64)
    return np.moveaxis((codes * scale).reshape(v.shape), -1, axis)


WIDE = False


def mx_kscale(k):
    if not WIDE:
        return np.ones(k)
    levels = np.array([30, -30])
    if k % 512:
        return np.exp2(np.random.permutation(np.resize(levels, k // 32))).repeat(32)
    a = np.empty((k // 512, 16))
    for p in range(k // 512):
        a[p, :8] = np.random.permutation(np.resize(levels, 8))
        for g in range(8):
            far = levels[np.abs(levels - a[p, g]) >= 10]
            a[p, g + 8] = far[np.random.randint(len(far))]
    return np.exp2(a.ravel()).repeat(32)


def f64(x):
    return np.asarray(x).astype(np.float64)


def striped(idx):
    return np.tile(np.asarray(idx).reshape(-1, 16).T, (8, 1)).astype(np.uint16)


def unstriped(offs):
    return offs[:16].T.reshape(-1).astype(np.int64)


E2M1 = np.array([0.0, 0.5, 1.0, 1.5, 2.0, 3.0, 4.0, 6.0, -0.0, -0.5, -1.0, -1.5, -2.0, -3.0, -4.0, -6.0])


def pack_weight(w, fmt):
    k, n = w.shape
    w = f64(np.asarray(w, np.float32).astype(ml_dtypes.bfloat16)).reshape(k // 32, 32, n)
    amax = np.abs(w).max(1)
    if fmt in ("e4m3", "e5m2"):
        byte = np.frexp(amax)[1] - 1 + 127 - (7 if fmt == "e4m3" else 14)
    else:
        mant, ex = np.frexp(amax / 6.0)
        byte = np.where(mant > 0.5, ex, ex - 1) + 127
    byte = np.clip(np.where(amax > 0, byte, 1), 1, 254)
    scaled = (w * np.exp2(127.0 - byte)[:, None, :]).reshape(k, n).astype(np.float32)
    by_word = np.ascontiguousarray(scaled.reshape(k // 512, 128, 4, n).transpose(0, 1, 3, 2))
    if fmt in ("e4m3", "e5m2"):
        words = by_word.astype(ml_dtypes.float8_e4m3fn if fmt == "e4m3" else ml_dtypes.float8_e5m2).view(np.uint8)
    else:
        c = by_word.astype(ml_dtypes.float4_e2m1fn).view(np.uint8) & 0xF
        words = (c[..., 0::2] | (c[..., 1::2] << 4)).reshape(k // 512, 128, 2 * n)
    return np.ascontiguousarray(words), np.ascontiguousarray(byte.astype(np.uint8).reshape(k // 512, 16, n))


def unpack_weight(words, scales, fmt):
    g, _, n = scales.shape
    words = np.ascontiguousarray(words).reshape(g, 128, n, -1)
    if fmt in ("e4m3", "e5m2"):
        vals = words.view(ml_dtypes.float8_e4m3fn if fmt == "e4m3" else ml_dtypes.float8_e5m2).astype(np.float64)
    else:
        nib = np.empty((g, 128, n, 4), np.uint8)
        nib[..., 0::2] = words & 0xF
        nib[..., 1::2] = words >> 4
        vals = E2M1[nib]
    vals = vals * np.repeat(np.exp2(scales.astype(np.float64) - 127.0), 8, axis=1)[..., None]
    return vals.transpose(0, 1, 3, 2).reshape(g * 512, n)


K, T, J, R, Q, N, E = 512, 2048, 256, 512, 1024, 256, 128


def setup_inputs():
    n = np.random.standard_normal
    idx = np.random.permutation(T)[:J]
    idx2 = np.random.permutation(T)[:J]
    idx3 = np.random.permutation(Q)[:J]
    idx4 = np.random.permutation(J)[:E]
    idx5 = np.random.permutation(J)[:E]
    fk = mx_kscale(K)
    fr = mx_kscale(R)
    xtp = pack_weight(n((K, T)) / fk[:, None], "e4m3")
    wp = pack_weight(n((K, R)) * 1 / np.sqrt(K) * fk[:, None] * fr, "e2m1")
    wbp = pack_weight(n((R, N)) * 1 / np.sqrt(R) / fr[:, None], "e5m2")
    wsp = pack_weight(n((K, N)) * 1 / np.sqrt(K) * fk[:, None], "e5m2")
    return {
        "xt_words": xtp[0],
        "xt_scales": xtp[1],
        "w_words": wp[0],
        "w_scales": wp[1],
        "ta": (np.random.uniform(-2.0, 1.0, (R, Q))).astype(np.float32),
        "wb_words": wbp[0],
        "wb_scales": wbp[1],
        "ws_words": wsp[0],
        "ws_scales": wsp[1],
        "offs": striped(idx),
        "offs2": striped(idx2),
        "offs3": striped(idx3),
        "offs4": striped(idx4),
        "offs5": striped(idx5),
    }


def reference(xt_words, xt_scales, w_words, w_scales, ta, wb_words, wb_scales, ws_words, ws_scales, offs, offs2, offs3, offs4, offs5):
    idx = unstriped(offs)
    idx2 = unstriped(offs2)
    idx3 = unstriped(offs3)
    idx4 = unstriped(offs4)
    idx5 = unstriped(offs5)
    xtu = unpack_weight(xt_words, xt_scales, "e4m3")
    wu = unpack_weight(w_words, w_scales, "e2m1")
    wbu = unpack_weight(wb_words, wb_scales, "e5m2")
    wsu = unpack_weight(ws_words, ws_scales, "e5m2")
    xtidxg = xtu[:, idx]
    a = wu.T @ xtidxg
    xtidx2g = xtu[:, idx2]
    b = wu.T @ xtidx2g
    nm = -np.max(f64(ta), axis=1, keepdims=True)
    hid = np.abs(a - b) * np.exp(f64(ta)[:, idx3] + nm)
    hidq = mxq(hid, 0, "e4m3")
    p = wbu.T @ hidq + wsu.T @ xtidxg
    y = np.maximum(p[:, idx4], p[:, idx5])
    return y

@@ -1,0 +1,175 @@
+from contextlib import ExitStack
+
+import concourse.mybir as mybir
+
+K, T, J, R, Q, N, E = 512, 2048, 256, 512, 1024, 256, 128
+FLOPS = 2 * (2 * K * R * J + R * N * J + K * N * J)
+
+F32 = mybir.dt.float32
+BF16 = mybir.dt.bfloat16
+I32 = mybir.dt.int32
+U32 = mybir.dt.uint32
+U16 = mybir.dt.uint16
+U8 = mybir.dt.uint8
+E4M3 = mybir.dt.float8_e4m3fn_x4
+E5M2 = mybir.dt.float8_e5m2_x4
+E2M1 = mybir.dt.float4_e2m1fn_x4
+ALU = mybir.AluOpType
+ACT = mybir.ActivationFunctionType
+AX = mybir.AxisListType
+
+P = 128
+PACK = 4
+
+
+def load_scale_rows(queue, plane, scales):
+    for q in range(4):
+        queue.dma_start(out=plane[32 * q : 32 * q + 4, :].bitcast(I32), in_=scales[0, 4 * q : 4 * q + 4, :].bitcast(I32))
+
+
+def tile_list_tied_fading_skip_bestoftwo_kernel(
+    tc, xt_words, xt_scales, w_words, w_scales, ta, wb_words, wb_scales, ws_words, ws_scales,
+    offs, offs2, offs3, offs4, offs5, out,
+):
+    nc = tc.nc
+    with ExitStack() as ctx:
+        lists = ctx.enter_context(tc.tile_pool(name="lists", bufs=1))
+        sb = ctx.enter_context(tc.tile_pool(name="sb", bufs=1))
+        ps = ctx.enter_context(tc.psum_pool(name="ps", bufs=1))
+
+        def tile(name, shape, dtype):
+            return sb.tile(shape, dtype, name=name, align_bytes=64)
+
+        l1 = lists.tile([P, J // 16], U16, name="l1")
+        l2 = lists.tile([P, J // 16], U16, name="l2")
+        l3 = lists.tile([P, J // 16], U16, name="l3")
+        l4 = lists.tile([P, E // 16], U16, name="l4")
+        l5 = lists.tile([P, E // 16], U16, name="l5")
+
+        xt_w = tile("xt_w", [P, T], I32)
+        xt_s = tile("xt_s", [P, T], U8)
+        w_raw = tile("w_raw", [P, R // 2], I32)
+        w_raw_s = tile("w_raw_s", [P, R], U8)
+        wb_w = tile("wb_w", [P, N], I32)
+        ws_w = tile("ws_w", [P, N], I32)
+        out_s = tile("out_s", [P, 2 * N], U8)
+        levels = [tile(f"levels{t}", [P, Q], F32) for t in range(PACK)]
+
+        nc.vector.memset(xt_s[:].bitcast(I32), 0)
+        nc.vector.memset(w_raw_s[:].bitcast(I32), 0)
+        nc.vector.memset(out_s[:].bitcast(I32), 0)
+
+        ta_rows = ta.rearrange("(p t) q -> t p q", t=PACK)
+        nc.sync.dma_start(l2[:], offs2)
+        nc.sync.dma_start(l1[:], offs)
+        nc.sync.dma_start(out=w_raw[:], in_=w_words[0].bitcast(I32))
+        load_scale_rows(nc.scalar, xt_s, xt_scales)
+        nc.sync.dma_start(out=xt_w[:], in_=xt_words[0].rearrange("p c r -> p (c r)").bitcast(I32))
+        load_scale_rows(nc.scalar, w_raw_s, w_scales)
+        nc.sync.dma_start(out=levels[0][:], in_=ta_rows[0])
+        nc.sync.dma_start(l3[:], offs3)
+        for t in range(1, PACK):
+            nc.sync.dma_start(out=levels[t][:], in_=ta_rows[t])
+        nc.sync.dma_start(out=ws_w[:], in_=ws_words[0].rearrange("p c r -> p (c r)").bitcast(I32))
+        nc.sync.dma_start(out=wb_w[:], in_=wb_words[0].rearrange("p c r -> p (c r)").bitcast(I32))
+        load_scale_rows(nc.sync, out_s[:, 0:N], ws_scales)
+        load_scale_rows(nc.sync, out_s[:, N : 2 * N], wb_scales)
+        nc.sync.dma_start(l4[:], offs4)
+        nc.sync.dma_start(l5[:], offs5)
+
+        w_w = tile("w_w", [P, R], U16)
+        w_s = tile("w_s", [P, R], U8)
+        xa_w = tile("xa_w", [P, J], U32)
+        xb_w = tile("xb_w", [P, J], U32)
+        xa_s = tile("xa_s", [P, J], U8)
+        xb_s = tile("xb_s", [P, J], U8)
+
+        nc.vector.tensor_copy(
+            out=w_w[:].rearrange("p (t m) -> p t m", t=PACK),
+            in_=w_raw[:].bitcast(U16).rearrange("p (m t) -> p t m", t=PACK),
+        )
+        nc.vector.tensor_copy(out=xb_s[:], in_=xt_s[:].indirect(l2[:]))
+        nc.vector.tensor_copy(out=xa_s[:], in_=xt_s[:].indirect(l1[:]))
+        nc.vector.tensor_copy(
+            out=w_s[:].rearrange("p (t m) -> p t m", t=PACK),
+            in_=w_raw_s[:].rearrange("p (m t) -> p t m", t=PACK),
+        )
+        nc.vector.tensor_copy(out=xb_w[:], in_=xt_w[:].bitcast(U32).indirect(l2[:]))
+        nc.vector.tensor_copy(out=xa_w[:], in_=xt_w[:].bitcast(U32).indirect(l1[:]))
+
+        a_ps = [ps.tile([P, 2, J], F32, name=f"a_ps{u}") for u in range(2)]
+        b_ps = [ps.tile([P, 2, J], F32, name=f"b_ps{u}") for u in range(2)]
+        p_ps = [ps.tile([P, J], F32, name=f"p_ps{h}") for h in range(2)]
+
+        def first_product(dst, t, x_w, x_s):
+            cols = slice(P * t, P * (t + 1))
+            nc.tensor.matmul_mx(
+                out=dst, lhsT=w_w[:, cols].bitcast(E2M1), lhsT_scale=w_s[:, cols],
+                rhs=x_w[:].bitcast(E4M3), rhs_scale=x_s[:], start=True, stop=True,
+            )
+
+        for u in range(2):
+            for i in range(2):
+                first_product(b_ps[u][:, i, :], 2 * u + i, xb_w, xb_s)
+            for i in range(2):
+                first_product(a_ps[u][:, i, :], 2 * u + i, xa_w, xa_s)
+        for h in range(2):
+            nc.tensor.matmul_mx(
+                out=p_ps[h][:], lhsT=ws_w[:, P * h : P * (h + 1)].bitcast(E5M2), lhsT_scale=out_s[:, P * h : P * (h + 1)],
+                rhs=xa_w[:].bitcast(E4M3), rhs_scale=xa_s[:], start=True, stop=False,
+            )
+
+        fade = [tile(f"fade{u}", [P, 2, J], F32) for u in range(2)]
+        dist = [tile(f"dist{u}", [P, 2, J], F32) for u in range(2)]
+        hid = tile("hid", [P, J, PACK], BF16)
+
+        def fading(t):
+            neg_max = tile(f"neg_max{t}", [P, 1], F32)
+            nc.vector.reduce_max(out=neg_max[:], in_=levels[t][:], axis=AX.X, negate=True)
+            nc.scalar.activation(out=fade[t // 2][:, t % 2, :], in_=levels[t][:].indirect(l3[:]), func=ACT.Exp, bias=neg_max[:])
+
+        def distance(u):
+            b_sb = tile(f"b_sb{u}", [P, 2, J], F32)
+            diff = tile(f"diff{u}", [P, 2, J], F32)
+            nc.scalar.copy(out=b_sb[:], in_=b_ps[u][:])
+            nc.vector.tensor_tensor(out=diff[:], in0=a_ps[u][:], in1=b_sb[:], op=ALU.subtract)
+            nc.scalar.activation(out=dist[u][:], in_=diff[:], func=ACT.Abs)
+
+        fading(0)
+        distance(0)
+        fading(1)
+        distance(1)
+        fading(2)
+        fading(3)
+        for u in range(2):
+            nc.vector.tensor_tensor(
+                out=hid[:, :, 2 * u : 2 * u + 2],
+                in0=dist[u][:].rearrange("p t j -> p j t"),
+                in1=fade[u][:].rearrange("p t j -> p j t"),
+                op=ALU.mult,
+            )
+
+        hid_w = tile("hid_w", [P, J], U32)
+        hid_s = tile("hid_s", [P, J], U8)
+        nc.vector.quantize_mx(out=hid_w[:].bitcast(E4M3), scales=hid_s[:], in_=hid[:].rearrange("p j t -> p (j t)"))
+
+        for h in range(2):
+            nc.tensor.matmul_mx(
+                out=p_ps[h][:], lhsT=wb_w[:, P * h : P * (h + 1)].bitcast(E5M2),
+                lhsT_scale=out_s[:, N + P * h : N + P * (h + 1)],
+                rhs=hid_w[:].bitcast(E4M3), rhs_scale=hid_s[:], start=False, stop=True,
+            )
+
+        p_sb = [tile(f"p_sb{h}", [P, J], F32) for h in range(2)]
+        first = [tile(f"first{h}", [P, E], F32) for h in range(2)]
+        second = [tile(f"second{h}", [P, E], F32) for h in range(2)]
+        best = [tile(f"best{h}", [P, E], F32) for h in range(2)]
+        nc.vector.tensor_copy(out=p_sb[0][:], in_=p_ps[0][:])
+        nc.scalar.copy(out=p_sb[1][:], in_=p_ps[1][:])
+        nc.vector.tensor_copy(out=first[0][:], in_=p_sb[0][:].indirect(l4[:]))
+        nc.vector.tensor_copy(out=second[0][:], in_=p_sb[0][:].indirect(l5[:]))
+        nc.scalar.activation(out=first[1][:], in_=p_sb[1][:].indirect(l4[:]), func=ACT.Copy)
+        nc.scalar.activation(out=second[1][:], in_=p_sb[1][:].indirect(l5[:]), func=ACT.Copy)
+        for h in range(2):
+            nc.vector.tensor_tensor(out=best[h][:], in0=first[h][:], in1=second[h][:], op=ALU.max)
+            nc.sync.dma_start(out=out[P * h : P * (h + 1), :], in_=best[h][:])

@@ -56,16 +56,16 @@ def tile_list_tied_fading_skip_bestoftwo_kernel(
         levels = [tile(f"levels{t}", [P, Q], F32) for t in range(PACK)]
 
         nc.vector.memset(xt_s[:].bitcast(I32), 0)
-        nc.vector.memset(w_raw_s[:].bitcast(I32), 0)
         nc.vector.memset(out_s[:].bitcast(I32), 0)
+        nc.vector.memset(w_raw_s[:].bitcast(I32), 0)
 
         ta_rows = ta.rearrange("(p t) q -> t p q", t=PACK)
         nc.sync.dma_start(l2[:], offs2)
         nc.sync.dma_start(l1[:], offs)
         nc.sync.dma_start(out=w_raw[:], in_=w_words[0].bitcast(I32))
-        load_scale_rows(nc.scalar, xt_s, xt_scales)
+        load_scale_rows(nc.sync, xt_s, xt_scales)
         nc.sync.dma_start(out=xt_w[:], in_=xt_words[0].rearrange("p c r -> p (c r)").bitcast(I32))
-        load_scale_rows(nc.scalar, w_raw_s, w_scales)
+        load_scale_rows(nc.sync, w_raw_s, w_scales)
         nc.sync.dma_start(out=levels[0][:], in_=ta_rows[0])
         nc.sync.dma_start(l3[:], offs3)
         for t in range(1, PACK):
@@ -90,11 +90,11 @@ def tile_list_tied_fading_skip_bestoftwo_kernel(
         )
         nc.vector.tensor_copy(out=xb_s[:], in_=xt_s[:].indirect(l2[:]))
         nc.vector.tensor_copy(out=xa_s[:], in_=xt_s[:].indirect(l1[:]))
+        nc.vector.tensor_copy(out=xb_w[:], in_=xt_w[:].bitcast(U32).indirect(l2[:]))
         nc.vector.tensor_copy(
             out=w_s[:].rearrange("p (t m) -> p t m", t=PACK),
             in_=w_raw_s[:].rearrange("p (m t) -> p t m", t=PACK),
         )
-        nc.vector.tensor_copy(out=xb_w[:], in_=xt_w[:].bitcast(U32).indirect(l2[:]))
         nc.vector.tensor_copy(out=xa_w[:], in_=xt_w[:].bitcast(U32).indirect(l1[:]))
 
         a_ps = [ps.tile([P, 2, J], F32, name=f"a_ps{u}") for u in range(2)]
@@ -141,35 +141,44 @@ def tile_list_tied_fading_skip_bestoftwo_kernel(
         distance(1)
         fading(2)
         fading(3)
-        for u in range(2):
+
+        def product(u, cols):
             nc.vector.tensor_tensor(
-                out=hid[:, :, 2 * u : 2 * u + 2],
-                in0=dist[u][:].rearrange("p t j -> p j t"),
-                in1=fade[u][:].rearrange("p t j -> p j t"),
+                out=hid[:, cols, 2 * u : 2 * u + 2],
+                in0=dist[u][:, :, cols].rearrange("p t j -> p j t"),
+                in1=fade[u][:, :, cols].rearrange("p t j -> p j t"),
                 op=ALU.mult,
             )
 
+        halves = [slice(0, J // 2), slice(J // 2, J)]
+        product(0, slice(0, J))
+        for cols in halves:
+            product(1, cols)
+
         hid_w = tile("hid_w", [P, J], U32)
         hid_s = tile("hid_s", [P, J], U8)
-        nc.vector.quantize_mx(out=hid_w[:].bitcast(E4M3), scales=hid_s[:], in_=hid[:].rearrange("p j t -> p (j t)"))
-
-        for h in range(2):
-            nc.tensor.matmul_mx(
-                out=p_ps[h][:], lhsT=wb_w[:, P * h : P * (h + 1)].bitcast(E5M2),
-                lhsT_scale=out_s[:, N + P * h : N + P * (h + 1)],
-                rhs=hid_w[:].bitcast(E4M3), rhs_scale=hid_s[:], start=False, stop=True,
+        for cols in halves:
+            nc.vector.quantize_mx(
+                out=hid_w[:, cols].bitcast(E4M3), scales=hid_s[:, cols], in_=hid[:, cols, :].rearrange("p j t -> p (j t)")
             )
+        for g, cols in enumerate(halves):
+            for h in range(2):
+                nc.tensor.matmul_mx(
+                    out=p_ps[h][:, cols], lhsT=wb_w[:, P * h : P * (h + 1)].bitcast(E5M2),
+                    lhsT_scale=out_s[:, N + P * h : N + P * (h + 1)],
+                    rhs=hid_w[:, cols].bitcast(E4M3), rhs_scale=hid_s[:, cols], start=False, stop=(g == 1),
+                )
 
         p_sb = [tile(f"p_sb{h}", [P, J], F32) for h in range(2)]
         first = [tile(f"first{h}", [P, E], F32) for h in range(2)]
         second = [tile(f"second{h}", [P, E], F32) for h in range(2)]
         best = [tile(f"best{h}", [P, E], F32) for h in range(2)]
-        nc.vector.tensor_copy(out=p_sb[0][:], in_=p_ps[0][:])
-        nc.scalar.copy(out=p_sb[1][:], in_=p_ps[1][:])
-        nc.vector.tensor_copy(out=first[0][:], in_=p_sb[0][:].indirect(l4[:]))
-        nc.vector.tensor_copy(out=second[0][:], in_=p_sb[0][:].indirect(l5[:]))
-        nc.scalar.activation(out=first[1][:], in_=p_sb[1][:].indirect(l4[:]), func=ACT.Copy)
-        nc.scalar.activation(out=second[1][:], in_=p_sb[1][:].indirect(l5[:]), func=ACT.Copy)
+        nc.scalar.copy(out=p_sb[0][:], in_=p_ps[0][:])
+        nc.vector.tensor_copy(out=p_sb[1][:], in_=p_ps[1][:])
+        nc.scalar.activation(out=first[0][:], in_=p_sb[0][:].indirect(l4[:]), func=ACT.Copy)
+        nc.scalar.activation(out=second[0][:], in_=p_sb[0][:].indirect(l5[:]), func=ACT.Copy)
+        nc.vector.tensor_copy(out=first[1][:], in_=p_sb[1][:].indirect(l4[:]))
+        nc.vector.tensor_copy(out=second[1][:], in_=p_sb[1][:].indirect(l5[:]))
         for h in range(2):
             nc.vector.tensor_tensor(out=best[h][:], in0=first[h][:], in1=second[h][:], op=ALU.max)
             nc.sync.dma_start(out=out[P * h : P * (h + 1), :], in_=best[h][:])

@@ -22,8 +22,8 @@ P = 128
 PACK = 4
 
 
-def load_scale_rows(queue, plane, scales):
-    for q in range(4):
+def load_scale_rows(queue, plane, scales, quadrants=range(4)):
+    for q in quadrants:
         queue.dma_start(out=plane[32 * q : 32 * q + 4, :].bitcast(I32), in_=scales[0, 4 * q : 4 * q + 4, :].bitcast(I32))
 
 
@@ -37,8 +37,8 @@ def tile_list_tied_fading_skip_bestoftwo_kernel(
         sb = ctx.enter_context(tc.tile_pool(name="sb", bufs=1))
         ps = ctx.enter_context(tc.psum_pool(name="ps", bufs=1))
 
-        def tile(name, shape, dtype):
-            return sb.tile(shape, dtype, name=name, align_bytes=64)
+        def tile(name, shape, dtype, tag=None):
+            return sb.tile(shape, dtype, name=name, tag=tag or name, align_bytes=64)
 
         l1 = lists.tile([P, J // 16], U16, name="l1")
         l2 = lists.tile([P, J // 16], U16, name="l2")
@@ -60,15 +60,18 @@ def tile_list_tied_fading_skip_bestoftwo_kernel(
         nc.vector.memset(w_raw_s[:].bitcast(I32), 0)
 
         ta_rows = ta.rearrange("(p t) q -> t p q", t=PACK)
+        nc.scalar.dma_start(out=levels[0][:], in_=ta_rows[0])
         nc.sync.dma_start(l2[:], offs2)
         nc.sync.dma_start(l1[:], offs)
-        nc.sync.dma_start(out=w_raw[:], in_=w_words[0].bitcast(I32))
-        load_scale_rows(nc.sync, xt_s, xt_scales)
+        load_scale_rows(nc.sync, xt_s, xt_scales, (0, 1))
+        load_scale_rows(nc.scalar, xt_s, xt_scales, (2, 3))
         nc.sync.dma_start(out=xt_w[:], in_=xt_words[0].rearrange("p c r -> p (c r)").bitcast(I32))
-        load_scale_rows(nc.sync, w_raw_s, w_scales)
-        nc.sync.dma_start(out=levels[0][:], in_=ta_rows[0])
+        nc.sync.dma_start(out=w_raw[:], in_=w_words[0].bitcast(I32))
+        load_scale_rows(nc.scalar, w_raw_s, w_scales, (0, 1, 2))
+        load_scale_rows(nc.sync, w_raw_s, w_scales, (3,))
+        nc.sync.dma_start(out=levels[1][:], in_=ta_rows[1])
         nc.sync.dma_start(l3[:], offs3)
-        for t in range(1, PACK):
+        for t in range(2, PACK):
             nc.sync.dma_start(out=levels[t][:], in_=ta_rows[t])
         nc.sync.dma_start(out=ws_w[:], in_=ws_words[0].rearrange("p c r -> p (c r)").bitcast(I32))
         nc.sync.dma_start(out=wb_w[:], in_=wb_words[0].rearrange("p c r -> p (c r)").bitcast(I32))
@@ -79,22 +82,30 @@ def tile_list_tied_fading_skip_bestoftwo_kernel(
 
         w_w = tile("w_w", [P, R], U16)
         w_s = tile("w_s", [P, R], U8)
-        xa_w = tile("xa_w", [P, J], U32)
         xb_w = tile("xb_w", [P, J], U32)
         xa_s = tile("xa_s", [P, J], U8)
         xb_s = tile("xb_s", [P, J], U8)
 
-        nc.vector.tensor_copy(
+        fade = [tile(f"fade{u}", [P, 2, J], F32) for u in range(2)]
+
+        def fading(t):
+            neg_max = tile(f"neg_max{t}", [P, 1], F32, tag="xt_w" if t == 1 else None)
+            nc.vector.reduce_max(out=neg_max[:], in_=levels[t][:], axis=AX.X, negate=True)
+            nc.scalar.activation(out=fade[t // 2][:, t % 2, :], in_=levels[t][:].indirect(l3[:]), func=ACT.Exp, bias=neg_max[:])
+
+        fading(0)
+        nc.vector.tensor_copy(out=xb_s[:], in_=xt_s[:].indirect(l2[:]))
+        nc.vector.tensor_copy(out=xa_s[:], in_=xt_s[:].indirect(l1[:]))
+        nc.scalar.copy(
             out=w_w[:].rearrange("p (t m) -> p t m", t=PACK),
             in_=w_raw[:].bitcast(U16).rearrange("p (m t) -> p t m", t=PACK),
         )
-        nc.vector.tensor_copy(out=xb_s[:], in_=xt_s[:].indirect(l2[:]))
-        nc.vector.tensor_copy(out=xa_s[:], in_=xt_s[:].indirect(l1[:]))
         nc.vector.tensor_copy(out=xb_w[:], in_=xt_w[:].bitcast(U32).indirect(l2[:]))
         nc.vector.tensor_copy(
             out=w_s[:].rearrange("p (t m) -> p t m", t=PACK),
             in_=w_raw_s[:].rearrange("p (m t) -> p t m", t=PACK),
         )
+        xa_w = tile("xa_w", [P, J], U32, tag="w_raw_s")
         nc.vector.tensor_copy(out=xa_w[:], in_=xt_w[:].bitcast(U32).indirect(l1[:]))
 
         a_ps = [ps.tile([P, 2, J], F32, name=f"a_ps{u}") for u in range(2)]
@@ -119,28 +130,23 @@ def tile_list_tied_fading_skip_bestoftwo_kernel(
                 rhs=xa_w[:].bitcast(E4M3), rhs_scale=xa_s[:], start=True, stop=False,
             )
 
-        fade = [tile(f"fade{u}", [P, 2, J], F32) for u in range(2)]
         dist = [tile(f"dist{u}", [P, 2, J], F32) for u in range(2)]
         hid = tile("hid", [P, J, PACK], BF16)
 
-        def fading(t):
-            neg_max = tile(f"neg_max{t}", [P, 1], F32)
-            nc.vector.reduce_max(out=neg_max[:], in_=levels[t][:], axis=AX.X, negate=True)
-            nc.scalar.activation(out=fade[t // 2][:, t % 2, :], in_=levels[t][:].indirect(l3[:]), func=ACT.Exp, bias=neg_max[:])
+        b_sb = [tile(f"b_sb{u}", [P, 2, J], F32) for u in range(2)]
+        for u in range(2):
+            nc.scalar.copy(out=b_sb[u][:], in_=b_ps[u][:])
 
         def distance(u):
-            b_sb = tile(f"b_sb{u}", [P, 2, J], F32)
             diff = tile(f"diff{u}", [P, 2, J], F32)
-            nc.scalar.copy(out=b_sb[:], in_=b_ps[u][:])
-            nc.vector.tensor_tensor(out=diff[:], in0=a_ps[u][:], in1=b_sb[:], op=ALU.subtract)
+            nc.vector.tensor_tensor(out=diff[:], in0=a_ps[u][:], in1=b_sb[u][:], op=ALU.subtract)
             nc.scalar.activation(out=dist[u][:], in_=diff[:], func=ACT.Abs)
 
-        fading(0)
-        distance(0)
         fading(1)
-        distance(1)
         fading(2)
+        distance(0)
         fading(3)
+        distance(1)
 
         def product(u, cols):
             nc.vector.tensor_tensor(
@@ -175,10 +181,10 @@ def tile_list_tied_fading_skip_bestoftwo_kernel(
         best = [tile(f"best{h}", [P, E], F32) for h in range(2)]
         nc.scalar.copy(out=p_sb[0][:], in_=p_ps[0][:])
         nc.vector.tensor_copy(out=p_sb[1][:], in_=p_ps[1][:])
-        nc.scalar.activation(out=first[0][:], in_=p_sb[0][:].indirect(l4[:]), func=ACT.Copy)
-        nc.scalar.activation(out=second[0][:], in_=p_sb[0][:].indirect(l5[:]), func=ACT.Copy)
-        nc.vector.tensor_copy(out=first[1][:], in_=p_sb[1][:].indirect(l4[:]))
-        nc.vector.tensor_copy(out=second[1][:], in_=p_sb[1][:].indirect(l5[:]))
+        for h in (1, 0):
+            nc.scalar.activation(out=first[h][:], in_=p_sb[h][:].indirect(l4[:]), func=ACT.Copy)
+        for h in (0, 1):
+            nc.vector.tensor_copy(out=second[h][:], in_=p_sb[h][:].indirect(l5[:]))
         for h in range(2):
             nc.vector.tensor_tensor(out=best[h][:], in0=first[h][:], in1=second[h][:], op=ALU.max)
             nc.sync.dma_start(out=out[P * h : P * (h + 1), :], in_=best[h][:])

@@ -22,9 +22,10 @@ P = 128
 PACK = 4
 
 
-def load_scale_rows(queue, plane, scales, quadrants=range(4)):
-    for q in quadrants:
-        queue.dma_start(out=plane[32 * q : 32 * q + 4, :].bitcast(I32), in_=scales[0, 4 * q : 4 * q + 4, :].bitcast(I32))
+def load_scale_rows(queue, plane, scales):
+    rows = scales[0].bitcast(I32).rearrange("(q r) c -> r q c", r=4)
+    for r in range(4):
+        queue.dma_start(out=plane.bitcast(I32)[r:P:32, :], in_=rows[r])
 
 
 def tile_list_tied_fading_skip_bestoftwo_kernel(
@@ -60,19 +61,17 @@ def tile_list_tied_fading_skip_bestoftwo_kernel(
         nc.vector.memset(w_raw_s[:].bitcast(I32), 0)
 
         ta_rows = ta.rearrange("(p t) q -> t p q", t=PACK)
-        nc.scalar.dma_start(out=levels[0][:], in_=ta_rows[0])
         nc.sync.dma_start(l2[:], offs2)
         nc.sync.dma_start(l1[:], offs)
-        load_scale_rows(nc.sync, xt_s, xt_scales, (0, 1))
-        load_scale_rows(nc.scalar, xt_s, xt_scales, (2, 3))
+        nc.sync.dma_start(out=levels[0][:], in_=ta_rows[0])
+        load_scale_rows(nc.sync, xt_s[:], xt_scales)
         nc.sync.dma_start(out=xt_w[:], in_=xt_words[0].rearrange("p c r -> p (c r)").bitcast(I32))
         nc.sync.dma_start(out=w_raw[:], in_=w_words[0].bitcast(I32))
-        load_scale_rows(nc.scalar, w_raw_s, w_scales, (0, 1, 2))
-        load_scale_rows(nc.sync, w_raw_s, w_scales, (3,))
-        nc.sync.dma_start(out=levels[1][:], in_=ta_rows[1])
-        nc.sync.dma_start(l3[:], offs3)
-        for t in range(2, PACK):
+        load_scale_rows(nc.sync, w_raw_s[:], w_scales)
+        for t in (1, 2):
             nc.sync.dma_start(out=levels[t][:], in_=ta_rows[t])
+        nc.sync.dma_start(l3[:], offs3)
+        nc.sync.dma_start(out=levels[3][:], in_=ta_rows[3])
         nc.sync.dma_start(out=ws_w[:], in_=ws_words[0].rearrange("p c r -> p (c r)").bitcast(I32))
         nc.sync.dma_start(out=wb_w[:], in_=wb_words[0].rearrange("p c r -> p (c r)").bitcast(I32))
         load_scale_rows(nc.sync, out_s[:, 0:N], ws_scales)
@@ -144,8 +143,8 @@ def tile_list_tied_fading_skip_bestoftwo_kernel(
 
         fading(1)
         fading(2)
-        distance(0)
         fading(3)
+        distance(0)
         distance(1)
 
         def product(u, cols):

@@ -63,15 +63,14 @@ def tile_list_tied_fading_skip_bestoftwo_kernel(
         ta_rows = ta.rearrange("(p t) q -> t p q", t=PACK)
         nc.sync.dma_start(l2[:], offs2)
         nc.sync.dma_start(l1[:], offs)
-        nc.sync.dma_start(out=levels[0][:], in_=ta_rows[0])
+        nc.sync.dma_start(out=w_raw[:], in_=w_words[0].bitcast(I32))
         load_scale_rows(nc.sync, xt_s[:], xt_scales)
         nc.sync.dma_start(out=xt_w[:], in_=xt_words[0].rearrange("p c r -> p (c r)").bitcast(I32))
-        nc.sync.dma_start(out=w_raw[:], in_=w_words[0].bitcast(I32))
         load_scale_rows(nc.sync, w_raw_s[:], w_scales)
-        for t in (1, 2):
-            nc.sync.dma_start(out=levels[t][:], in_=ta_rows[t])
+        nc.sync.dma_start(out=levels[0][:], in_=ta_rows[0])
         nc.sync.dma_start(l3[:], offs3)
-        nc.sync.dma_start(out=levels[3][:], in_=ta_rows[3])
+        for t in range(1, PACK):
+            nc.sync.dma_start(out=levels[t][:], in_=ta_rows[t])
         nc.sync.dma_start(out=ws_w[:], in_=ws_words[0].rearrange("p c r -> p (c r)").bitcast(I32))
         nc.sync.dma_start(out=wb_w[:], in_=wb_words[0].rearrange("p c r -> p (c r)").bitcast(I32))
         load_scale_rows(nc.sync, out_s[:, 0:N], ws_scales)
@@ -88,17 +87,16 @@ def tile_list_tied_fading_skip_bestoftwo_kernel(
         fade = [tile(f"fade{u}", [P, 2, J], F32) for u in range(2)]
 
         def fading(t):
-            neg_max = tile(f"neg_max{t}", [P, 1], F32, tag="xt_w" if t == 1 else None)
+            neg_max = tile(f"neg_max{t}", [P, 1], F32)
             nc.vector.reduce_max(out=neg_max[:], in_=levels[t][:], axis=AX.X, negate=True)
             nc.scalar.activation(out=fade[t // 2][:, t % 2, :], in_=levels[t][:].indirect(l3[:]), func=ACT.Exp, bias=neg_max[:])
 
-        fading(0)
-        nc.vector.tensor_copy(out=xb_s[:], in_=xt_s[:].indirect(l2[:]))
-        nc.vector.tensor_copy(out=xa_s[:], in_=xt_s[:].indirect(l1[:]))
-        nc.scalar.copy(
+        nc.vector.tensor_copy(
             out=w_w[:].rearrange("p (t m) -> p t m", t=PACK),
             in_=w_raw[:].bitcast(U16).rearrange("p (m t) -> p t m", t=PACK),
         )
+        nc.vector.tensor_copy(out=xb_s[:], in_=xt_s[:].indirect(l2[:]))
+        nc.vector.tensor_copy(out=xa_s[:], in_=xt_s[:].indirect(l1[:]))
         nc.vector.tensor_copy(out=xb_w[:], in_=xt_w[:].bitcast(U32).indirect(l2[:]))
         nc.vector.tensor_copy(
             out=w_s[:].rearrange("p (t m) -> p t m", t=PACK),
@@ -129,23 +127,20 @@ def tile_list_tied_fading_skip_bestoftwo_kernel(
                 rhs=xa_w[:].bitcast(E4M3), rhs_scale=xa_s[:], start=True, stop=False,
             )
 
-        dist = [tile(f"dist{u}", [P, 2, J], F32) for u in range(2)]
-        hid = tile("hid", [P, J, PACK], BF16)
-
+        diff = [tile(f"diff{u}", [P, 2, J], F32) for u in range(2)]
         b_sb = [tile(f"b_sb{u}", [P, 2, J], F32) for u in range(2)]
+        a_sb = tile("a_sb", [P, 2, J], F32)
+        nc.scalar.copy(out=b_sb[0][:], in_=b_ps[0][:])
+        nc.scalar.copy(out=a_sb[:], in_=a_ps[0][:])
+        nc.scalar.copy(out=b_sb[1][:], in_=b_ps[1][:])
+        nc.gpsimd.tensor_tensor(out=diff[0][:], in0=a_sb[:], in1=b_sb[0][:], op=ALU.subtract)
+        for t in range(PACK):
+            fading(t)
+        nc.vector.tensor_tensor(out=diff[1][:], in0=a_ps[1][:], in1=b_sb[1][:], op=ALU.subtract)
+        dist = [tile("dist0", [P, 2, J], F32, tag="levels1"), tile("dist1", [P, 2, J], F32)]
         for u in range(2):
-            nc.scalar.copy(out=b_sb[u][:], in_=b_ps[u][:])
-
-        def distance(u):
-            diff = tile(f"diff{u}", [P, 2, J], F32)
-            nc.vector.tensor_tensor(out=diff[:], in0=a_ps[u][:], in1=b_sb[u][:], op=ALU.subtract)
-            nc.scalar.activation(out=dist[u][:], in_=diff[:], func=ACT.Abs)
-
-        fading(1)
-        fading(2)
-        fading(3)
-        distance(0)
-        distance(1)
+            nc.scalar.activation(out=dist[u][:], in_=diff[u][:], func=ACT.Abs)
+        hid = tile("hid", [P, J, PACK], BF16, tag="levels2")
 
         def product(u, cols):
             nc.vector.tensor_tensor(

from contextlib import ExitStack

import concourse.mybir as mybir

K, T, J, R, Q, N, E = 512, 2048, 256, 512, 1024, 256, 128
FLOPS = 2 * (2 * K * R * J + R * N * J + K * N * J)

F32 = mybir.dt.float32
BF16 = mybir.dt.bfloat16
I32 = mybir.dt.int32
U32 = mybir.dt.uint32
U16 = mybir.dt.uint16
U8 = mybir.dt.uint8
E4M3 = mybir.dt.float8_e4m3fn_x4
E5M2 = mybir.dt.float8_e5m2_x4
E2M1 = mybir.dt.float4_e2m1fn_x4
ALU = mybir.AluOpType
ACT = mybir.ActivationFunctionType
AX = mybir.AxisListType

P = 128
PACK = 4


def load_scale_rows(queue, plane, scales):
    rows = scales[0].bitcast(I32).rearrange("(q r) c -> r q c", r=4)
    for r in range(4):
        queue.dma_start(out=plane.bitcast(I32)[r:P:32, :], in_=rows[r])


def tile_list_tied_fading_skip_bestoftwo_kernel(
    tc, xt_words, xt_scales, w_words, w_scales, ta, wb_words, wb_scales, ws_words, ws_scales,
    offs, offs2, offs3, offs4, offs5, out,
):
    nc = tc.nc
    with ExitStack() as ctx:
        lists = ctx.enter_context(tc.tile_pool(name="lists", bufs=1))
        sb = ctx.enter_context(tc.tile_pool(name="sb", bufs=1))
        ps = ctx.enter_context(tc.psum_pool(name="ps", bufs=1))

        def tile(name, shape, dtype, tag=None):
            return sb.tile(shape, dtype, name=name, tag=tag or name, align_bytes=64)

        l1 = lists.tile([P, J // 16], U16, name="l1")
        l2 = lists.tile([P, J // 16], U16, name="l2")
        l3 = lists.tile([P, J // 16], U16, name="l3")
        l4 = lists.tile([P, E // 16], U16, name="l4")
        l5 = lists.tile([P, E // 16], U16, name="l5")

        xt_w = tile("xt_w", [P, T], I32)
        xt_s = tile("xt_s", [P, T], U8)
        w_raw = tile("w_raw", [P, R // 2], I32)
        w_raw_s = tile("w_raw_s", [P, R], U8)
        wb_w = tile("wb_w", [P, N], I32)
        ws_w = tile("ws_w", [P, N], I32)
        out_s = tile("out_s", [P, 2 * N], U8)
        levels = [tile(f"levels{t}", [P, Q], F32) for t in range(PACK)]

        nc.vector.memset(xt_s[:].bitcast(I32), 0)
        nc.vector.memset(out_s[:].bitcast(I32), 0)
        nc.vector.memset(w_raw_s[:].bitcast(I32), 0)

        ta_rows = ta.rearrange("(p t) q -> t p q", t=PACK)
        nc.sync.dma_start(l2[:], offs2)
        nc.sync.dma_start(l1[:], offs)
        nc.sync.dma_start(out=w_raw[:], in_=w_words[0].bitcast(I32))
        load_scale_rows(nc.sync, xt_s[:], xt_scales)
        nc.sync.dma_start(out=xt_w[:], in_=xt_words[0].rearrange("p c r -> p (c r)").bitcast(I32))
        load_scale_rows(nc.sync, w_raw_s[:], w_scales)
        nc.sync.dma_start(out=levels[0][:], in_=ta_rows[0])
        nc.sync.dma_start(l3[:], offs3)
        for t in range(1, PACK):
            nc.sync.dma_start(out=levels[t][:], in_=ta_rows[t])
        nc.sync.dma_start(out=ws_w[:], in_=ws_words[0].rearrange("p c r -> p (c r)").bitcast(I32))
        nc.sync.dma_start(out=wb_w[:], in_=wb_words[0].rearrange("p c r -> p (c r)").bitcast(I32))
        load_scale_rows(nc.sync, out_s[:, 0:N], ws_scales)
        load_scale_rows(nc.sync, out_s[:, N : 2 * N], wb_scales)
        nc.sync.dma_start(l4[:], offs4)
        nc.sync.dma_start(l5[:], offs5)

        w_w = tile("w_w", [P, R], U16)
        w_s = tile("w_s", [P, R], U8)
        xb_w = tile("xb_w", [P, J], U32)
        xa_s = tile("xa_s", [P, J], U8)
        xb_s = tile("xb_s", [P, J], U8)

        fade = [tile(f"fade{u}", [P, 2, J], F32) for u in range(2)]

        def fading(t):
            neg_max = tile(f"neg_max{t}", [P, 1], F32)
            nc.vector.reduce_max(out=neg_max[:], in_=levels[t][:], axis=AX.X, negate=True)
            nc.scalar.activation(out=fade[t // 2][:, t % 2, :], in_=levels[t][:].indirect(l3[:]), func=ACT.Exp, bias=neg_max[:])

        nc.vector.tensor_copy(
            out=w_w[:].rearrange("p (t m) -> p t m", t=PACK),
            in_=w_raw[:].bitcast(U16).rearrange("p (m t) -> p t m", t=PACK),
        )
        nc.vector.tensor_copy(out=xb_s[:], in_=xt_s[:].indirect(l2[:]))
        nc.vector.tensor_copy(out=xa_s[:], in_=xt_s[:].indirect(l1[:]))
        nc.vector.tensor_copy(out=xb_w[:], in_=xt_w[:].bitcast(U32).indirect(l2[:]))
        nc.vector.tensor_copy(
            out=w_s[:].rearrange("p (t m) -> p t m", t=PACK),
            in_=w_raw_s[:].rearrange("p (m t) -> p t m", t=PACK),
        )
        xa_w = tile("xa_w", [P, J], U32, tag="w_raw_s")
        nc.vector.tensor_copy(out=xa_w[:], in_=xt_w[:].bitcast(U32).indirect(l1[:]))

        a_ps = [ps.tile([P, 2, J], F32, name=f"a_ps{u}") for u in range(2)]
        b_ps = [ps.tile([P, 2, J], F32, name=f"b_ps{u}") for u in range(2)]
        p_ps = [ps.tile([P, J], F32, name=f"p_ps{h}") for h in range(2)]

        def first_product(dst, t, x_w, x_s):
            cols = slice(P * t, P * (t + 1))
            nc.tensor.matmul_mx(
                out=dst, lhsT=w_w[:, cols].bitcast(E2M1), lhsT_scale=w_s[:, cols],
                rhs=x_w[:].bitcast(E4M3), rhs_scale=x_s[:], start=True, stop=True,
            )

        for u in range(2):
            for i in range(2):
                first_product(b_ps[u][:, i, :], 2 * u + i, xb_w, xb_s)
            for i in range(2):
                first_product(a_ps[u][:, i, :], 2 * u + i, xa_w, xa_s)
        for h in range(2):
            nc.tensor.matmul_mx(
                out=p_ps[h][:], lhsT=ws_w[:, P * h : P * (h + 1)].bitcast(E5M2), lhsT_scale=out_s[:, P * h : P * (h + 1)],
                rhs=xa_w[:].bitcast(E4M3), rhs_scale=xa_s[:], start=True, stop=False,
            )

        diff = [tile(f"diff{u}", [P, 2, J], F32) for u in range(2)]
        b_sb = [tile(f"b_sb{u}", [P, 2, J], F32) for u in range(2)]
        a_sb = tile("a_sb", [P, 2, J], F32)
        nc.scalar.copy(out=b_sb[0][:], in_=b_ps[0][:])
        nc.scalar.copy(out=a_sb[:], in_=a_ps[0][:])
        nc.scalar.copy(out=b_sb[1][:], in_=b_ps[1][:])
        nc.gpsimd.tensor_tensor(out=diff[0][:], in0=a_sb[:], in1=b_sb[0][:], op=ALU.subtract)
        for t in range(PACK):
            fading(t)
        nc.vector.tensor_tensor(out=diff[1][:], in0=a_ps[1][:], in1=b_sb[1][:], op=ALU.subtract)
        dist = [tile("dist0", [P, 2, J], F32, tag="levels1"), tile("dist1", [P, 2, J], F32)]
        for u in range(2):
            nc.scalar.activation(out=dist[u][:], in_=diff[u][:], func=ACT.Abs)
        hid = tile("hid", [P, J, PACK], BF16, tag="levels2")

        def product(u, cols):
            nc.vector.tensor_tensor(
                out=hid[:, cols, 2 * u : 2 * u + 2],
                in0=dist[u][:, :, cols].rearrange("p t j -> p j t"),
                in1=fade[u][:, :, cols].rearrange("p t j -> p j t"),
                op=ALU.mult,
            )

        halves = [slice(0, J // 2), slice(J // 2, J)]
        product(0, slice(0, J))
        for cols in halves:
            product(1, cols)

        hid_w = tile("hid_w", [P, J], U32)
        hid_s = tile("hid_s", [P, J], U8)
        for cols in halves:
            nc.vector.quantize_mx(
                out=hid_w[:, cols].bitcast(E4M3), scales=hid_s[:, cols], in_=hid[:, cols, :].rearrange("p j t -> p (j t)")
            )
        for g, cols in enumerate(halves):
            for h in range(2):
                nc.tensor.matmul_mx(
                    out=p_ps[h][:, cols], lhsT=wb_w[:, P * h : P * (h + 1)].bitcast(E5M2),
                    lhsT_scale=out_s[:, N + P * h : N + P * (h + 1)],
                    rhs=hid_w[:, cols].bitcast(E4M3), rhs_scale=hid_s[:, cols], start=False, stop=(g == 1),
                )

        p_sb = [tile(f"p_sb{h}", [P, J], F32) for h in range(2)]
        first = [tile(f"first{h}", [P, E], F32) for h in range(2)]
        second = [tile(f"second{h}", [P, E], F32) for h in range(2)]
        best = [tile(f"best{h}", [P, E], F32) for h in range(2)]
        nc.scalar.copy(out=p_sb[0][:], in_=p_ps[0][:])
        nc.vector.tensor_copy(out=p_sb[1][:], in_=p_ps[1][:])
        for h in (1, 0):
            nc.scalar.activation(out=first[h][:], in_=p_sb[h][:].indirect(l4[:]), func=ACT.Copy)
        for h in (0, 1):
            nc.vector.tensor_copy(out=second[h][:], in_=p_sb[h][:].indirect(l5[:]))
        for h in range(2):
            nc.vector.tensor_tensor(out=best[h][:], in0=first[h][:], in1=second[h][:], op=ALU.max)
            nc.sync.dma_start(out=out[P * h : P * (h + 1), :], in_=best[h][:])
